import numpy as np
import ml_dtypes


def mxq(x, axis, fmt="e4m3"):
    dtype, down = {"e4m3": (ml_dtypes.float8_e4m3fn, 7), "e5m2": (ml_dtypes.float8_e5m2, 14)}[fmt]
    v = np.moveaxis(np.asarray(x, np.float32).astype(ml_dtypes.bfloat16).astype(np.float64), axis, -1)
    blocks = v.reshape(v.shape[:-1] + (-1, 32))
    amax = np.abs(blocks).max(-1, keepdims=True)
    byte = np.maximum(np.where(amax > 0, np.frexp(amax)[1] - 1 + 127, 0) - down, 1)
    scale = np.exp2(byte - 127.0)
    codes = (blocks / scale).astype(np.float32).astype(dtype).astype(np.float64)
    return np.moveaxis((codes * scale).reshape(v.shape), -1, axis)


WIDE = False


def mx_kscale(k):
    if not WIDE:
        return np.ones(k)
    levels = np.array([30, -30])
    if k % 512:
        return np.exp2(np.random.permutation(np.resize(levels, k // 32))).repeat(32)
    a = np.empty((k // 512, 16))
    for p in range(k // 512):
        a[p, :8] = np.random.permutation(np.resize(levels, 8))
        for g in range(8):
            far = levels[np.abs(levels - a[p, g]) >= 10]
            a[p, g + 8] = far[np.random.randint(len(far))]
    return np.exp2(a.ravel()).repeat(32)


def f64(x):
    return np.asarray(x).astype(np.float64)


def striped(idx):
    return np.tile(np.asarray(idx).reshape(-1, 16).T, (8, 1)).astype(np.uint16)


def unstriped(offs):
    return offs[:16].T.reshape(-1).astype(np.int64)


def striped8(idx):
    return np.asarray(idx).reshape(8, -1, 16).transpose(0, 2, 1).reshape(128, -1).astype(np.uint16)


def unstriped8(offs):
    return offs.reshape(8, 16, -1).transpose(0, 2, 1).reshape(8, -1).astype(np.int64)


def pick8(x, idx, run):
    r = np.arange(len(x))
    return x[r[:, None], idx[r % (8 * run) // run]]


E2M1 = np.array([0.0, 0.5, 1.0, 1.5, 2.0, 3.0, 4.0, 6.0, -0.0, -0.5, -1.0, -1.5, -2.0, -3.0, -4.0, -6.0])


def pack_weight(w, fmt):
    k, n = w.shape
    w = f64(np.asarray(w, np.float32).astype(ml_dtypes.bfloat16)).reshape(k // 32, 32, n)
    amax = np.abs(w).max(1)
    if fmt in ("e4m3", "e5m2"):
        byte = np.frexp(amax)[1] - 1 + 127 - (7 if fmt == "e4m3" else 14)
    else:
        mant, ex = np.frexp(amax / 6.0)
        byte = np.where(mant > 0.5, ex, ex - 1) + 127
    byte = np.clip(np.where(amax > 0, byte, 1), 1, 254)
    scaled = (w * np.exp2(127.0 - byte)[:, None, :]).reshape(k, n).astype(np.float32)
    by_word = np.ascontiguousarray(scaled.reshape(k // 512, 128, 4, n).transpose(0, 1, 3, 2))
    if fmt in ("e4m3", "e5m2"):
        words = by_word.astype(ml_dtypes.float8_e4m3fn if fmt == "e4m3" else ml_dtypes.float8_e5m2).view(np.uint8)
    else:
        c = by_word.astype(ml_dtypes.float4_e2m1fn).view(np.uint8) & 0xF
        words = (c[..., 0::2] | (c[..., 1::2] << 4)).reshape(k // 512, 128, 2 * n)
    return np.ascontiguousarray(words), np.ascontiguousarray(byte.astype(np.uint8).reshape(k // 512, 16, n))


def unpack_weight(words, scales, fmt):
    g, _, n = scales.shape
    words = np.ascontiguousarray(words).reshape(g, 128, n, -1)
    if fmt in ("e4m3", "e5m2"):
        vals = words.view(ml_dtypes.float8_e4m3fn if fmt == "e4m3" else ml_dtypes.float8_e5m2).astype(np.float64)
    else:
        nib = np.empty((g, 128, n, 4), np.uint8)
        nib[..., 0::2] = words & 0xF
        nib[..., 1::2] = words >> 4
        vals = E2M1[nib]
    vals = vals * np.repeat(np.exp2(scales.astype(np.float64) - 127.0), 8, axis=1)[..., None]
    return vals.transpose(0, 1, 3, 2).reshape(g * 512, n)


def sgn(shape):
    return np.random.uniform(0.5, 2.0, shape) * np.where(np.random.standard_normal(shape) < 0, -1.0, 1.0)


K, T, F, Z, J, N, E = 512, 512, 512, 1024, 256, 256, 512


def setup_inputs():
    n = np.random.standard_normal
    idx = np.stack([np.random.permutation(T)[:J] for _ in range(8)])
    idx2 = np.random.permutation(Z)[:J]
    idx3 = np.random.permutation(E)[:J]
    fk = mx_kscale(K)
    ff = mx_kscale(F)
    xop = pack_weight(n((F, Z)) / ff[:, None], "e2m1")
    wp = pack_weight(n((K, N)) * 1 / np.sqrt(K) / fk[:, None], "e2m1")
    w2p = pack_weight(n((F, N)) * 1 / np.sqrt(F) * ff[:, None], "e5m2")
    return {
        "ca": (np.random.randint(-7, 8, (K, T)).astype(np.float64)).astype(np.float32),
        "sa": (np.random.uniform(0.08, 0.3, (K, 1)) * fk[:, None]).astype(np.float32),
        "xo_words": xop[0],
        "xo_scales": xop[1],
        "w_words": wp[0],
        "w_scales": wp[1],
        "w2_words": w2p[0],
        "w2_scales": w2p[1],
        "so": (sgn((N, 1))).astype(np.float32),
        "offs": striped8(idx),
        "offs2": striped(idx2),
        "offs3": striped(idx3),
    }


def reference(ca, sa, xo_words, xo_scales, w_words, w_scales, w2_words, w2_scales, so, offs, offs2, offs3):
    idx = unstriped8(offs)
    idx2 = unstriped(offs2)
    idx3 = unstriped(offs3)
    xou = unpack_weight(xo_words, xo_scales, "e2m1")
    wu = unpack_weight(w_words, w_scales, "e2m1")
    w2u = unpack_weight(w2_words, w2_scales, "e5m2")
    z1 = pick8(f64(ca), idx, 64) * f64(sa)
    z1q = mxq(z1, 0, "e4m3")
    xoidx2g = xou[:, idx2]
    p = wu.T @ z1q + w2u.T @ xoidx2g
    y = np.zeros((N, E))
    y[:, idx3] = p * f64(so)
    return y

@@ -1,0 +1,132 @@
+from contextlib import ExitStack
+
+import concourse.mybir as mybir
+
+F32 = mybir.dt.float32
+BF16 = mybir.dt.bfloat16
+I32 = mybir.dt.int32
+U32 = mybir.dt.uint32
+U16 = mybir.dt.uint16
+U8 = mybir.dt.uint8
+E4M3X4 = mybir.dt.float8_e4m3fn_x4
+E5M2X4 = mybir.dt.float8_e5m2_x4
+E2M1X4 = mybir.dt.float4_e2m1fn_x4
+COPY = mybir.ActivationFunctionType.Copy
+
+P = 128
+PACK = 4
+K, T, F, Z, J, N, E = 512, 512, 512, 1024, 256, 256, 512
+HALF = J // 2
+LIST_COLS = J // 16
+FLOPS = 2 * K * N * J + 2 * F * N * J
+
+
+def tile_list_codesbeside_kernel(tc, ca, sa, xo_words, xo_scales, w_words, w_scales, w2_words, w2_scales, so, offs, offs2, offs3, out):
+    nc = tc.nc
+    with ExitStack() as ctx:
+        keep = ctx.enter_context(tc.tile_pool(name="keep", bufs=1))
+        psum = ctx.enter_context(tc.psum_pool(name="psum", bufs=1))
+
+        code_list = keep.tile([P, LIST_COLS], U16, name="code_list")
+        token_list = keep.tile([P, LIST_COLS], U16, name="token_list")
+        page_list = keep.tile([P, LIST_COLS], U16, name="page_list")
+        steps = keep.tile([P, PACK], F32, name="steps")
+        gains = keep.tile([P, N // P], F32, name="gains")
+        table = [keep.tile([P, T], F32, name=f"table{r}") for r in range(PACK)]
+        xo_all = keep.tile([P, Z], U16, name="xo_all", align_bytes=64)
+        w_codes = keep.tile([P, 2 * N], U8, name="w_codes", align_bytes=64)
+        w2_codes = keep.tile([P, N], I32, name="w2_codes", align_bytes=64)
+        xo_rows = keep.tile([4, 4, Z // 4], I32, name="xo_rows")
+        w_rows = keep.tile([4, 4, N // 4], I32, name="w_rows")
+        w2_rows = keep.tile([4, 4, N // 4], I32, name="w2_rows")
+        xo_plane_all = keep.tile([P, Z], U8, name="xo_plane_all", align_bytes=64)
+        w_plane = keep.tile([P, N], U8, name="w_plane", align_bytes=64)
+        w2_plane = keep.tile([P, N], U8, name="w2_plane", align_bytes=64)
+        pages = [keep.tile([P, E], F32, name=f"page{t}") for t in range(N // P)]
+
+        ca_planes = ca.rearrange("(p r) t -> r p t", r=PACK)
+
+        def scale_rows(src):
+            return src[0].bitcast(I32).rearrange("(q r) c -> r q c", r=4)
+
+        nc.scalar.dma_start(table[0][:], ca_planes[0])
+        nc.sync.dma_start(code_list[:], offs)
+        nc.sync.dma_start(steps[:], sa.rearrange("(p r) o -> p (r o)", r=PACK))
+        for r in range(1, PACK):
+            nc.sync.dma_start(table[r][:], ca_planes[r])
+        nc.sync.dma_start(xo_rows[:], scale_rows(xo_scales))
+        nc.sync.dma_start(token_list[:], offs2)
+        nc.sync.dma_start(xo_all[:].bitcast(I32), xo_words[0].bitcast(I32))
+        nc.sync.dma_start(w2_codes[:], w2_words[0].rearrange("p n t -> p (n t)").bitcast(I32))
+        nc.sync.dma_start(w_codes[:].bitcast(I32), w_words[0].bitcast(I32))
+        nc.sync.dma_start(page_list[:], offs3)
+        nc.gpsimd.dma_start(w2_rows[:], scale_rows(w2_scales))
+        nc.gpsimd.dma_start(w_rows[:], scale_rows(w_scales))
+        with nc.allow_non_contiguous_dma(reason="one gain a partition"):
+            nc.sync.dma_start(gains[:], so.rearrange("(t p) o -> p (t o)", p=P))
+
+        for plane in (xo_plane_all, w2_plane, w_plane):
+            nc.vector.memset(plane[:].bitcast(I32), 0)
+        for page in pages:
+            nc.gpsimd.memset(page[:], 0.0)
+
+        def spread(plane, rows):
+            for q in range(4):
+                nc.vector.tensor_copy(plane[32 * q : 32 * q + 4, :].bitcast(I32), rows[:, q, :])
+
+        spread(w2_plane, w2_rows)
+        spread(w_plane, w_rows)
+        spread(xo_plane_all, xo_rows)
+
+        xo_plane = keep.tile([P, J], U8, name="xo_plane", align_bytes=64)
+        nc.vector.tensor_copy(xo_plane[:], xo_plane_all[:].indirect(token_list[:]))
+
+        def half_list(lst, h):
+            return lst[:, h * LIST_COLS // 2 : (h + 1) * LIST_COLS // 2]
+
+        z = [keep.tile([P, PACK * HALF], BF16, name=f"z{h}", align_bytes=64) for h in range(2)]
+
+        def fetch(r, h):
+            nc.scalar.activation(
+                z[h][:, r : PACK * HALF : PACK], table[r][:].indirect(half_list(code_list, h)), COPY, scale=steps[:, r : r + 1]
+            )
+
+        for r, h in ((0, 0), (0, 1), (1, 0), (2, 0), (3, 0), (1, 1), (2, 1), (3, 1)):
+            fetch(r, h)
+
+        sums = {}
+        for h in range(2):
+            xo_codes = keep.tile([P, HALF], U16, name=f"xo_codes{h}", align_bytes=64)
+            nc.vector.tensor_copy(xo_codes[:], xo_all[:].indirect(half_list(token_list, h)))
+            z_codes = keep.tile([P, HALF], U32, name=f"z_codes{h}", align_bytes=64)
+            z_plane = keep.tile([P, HALF], U8, name=f"z_plane{h}", align_bytes=64)
+            nc.vector.quantize_mx(out=z_codes[:].bitcast(E4M3X4), scales=z_plane[:], in_=z[h][:])
+            for t in range(N // P):
+                acc = psum.tile([P, HALF], F32, name=f"acc{h}{t}")
+                nc.tensor.matmul_mx(
+                    out=acc[:],
+                    lhsT=w2_codes[:, t * P : (t + 1) * P].bitcast(E5M2X4),
+                    lhsT_scale=w2_plane[:, t * P : (t + 1) * P],
+                    rhs=xo_codes[:].bitcast(E2M1X4),
+                    rhs_scale=xo_plane[:, h * HALF : (h + 1) * HALF],
+                    start=True,
+                    stop=False,
+                )
+                nc.tensor.matmul_mx(
+                    out=acc[:],
+                    lhsT=w_codes[:, 2 * t * P : 2 * (t + 1) * P].bitcast(E2M1X4),
+                    lhsT_scale=w_plane[:, t * P : (t + 1) * P],
+                    rhs=z_codes[:].bitcast(E4M3X4),
+                    rhs_scale=z_plane[:],
+                    start=False,
+                    stop=True,
+                )
+                p_rows = keep.tile([P, HALF], F32, name=f"p_rows{h}{t}")
+                nc.vector.tensor_copy(p_rows[:], acc[:])
+                sums[h, t] = p_rows
+
+        for h in range(2):
+            for t in range(N // P):
+                nc.scalar.activation(pages[t][:].indirect(half_list(page_list, h)), sums[h, t][:], COPY, scale=gains[:, t : t + 1])
+        for t in range(N // P):
+            nc.sync.dma_start(out[t * P : (t + 1) * P, :], pages[t][:])

@@ -36,47 +36,53 @@ def tile_list_codesbeside_kernel(tc, ca, sa, xo_words, xo_scales, w_words, w_sca
         xo_all = keep.tile([P, Z], U16, name="xo_all", align_bytes=64)
         w_codes = keep.tile([P, 2 * N], U8, name="w_codes", align_bytes=64)
         w2_codes = keep.tile([P, N], I32, name="w2_codes", align_bytes=64)
-        xo_rows = keep.tile([4, 4, Z // 4], I32, name="xo_rows")
-        w_rows = keep.tile([4, 4, N // 4], I32, name="w_rows")
-        w2_rows = keep.tile([4, 4, N // 4], I32, name="w2_rows")
+        xo_rows = keep.tile([64, 2, Z // 4], I32, name="xo_rows")
         xo_plane_all = keep.tile([P, Z], U8, name="xo_plane_all", align_bytes=64)
-        w_plane = keep.tile([P, N], U8, name="w_plane", align_bytes=64)
-        w2_plane = keep.tile([P, N], U8, name="w2_plane", align_bytes=64)
+        w_plane = keep.tile([P, 2 * N], U8, name="w_plane", align_bytes=64)
+        w2_plane = keep.tile([P, 2 * N], U8, name="w2_plane", align_bytes=64)
         pages = [keep.tile([P, E], F32, name=f"page{t}") for t in range(N // P)]
 
         ca_planes = ca.rearrange("(p r) t -> r p t", r=PACK)
 
-        def scale_rows(src):
-            return src[0].bitcast(I32).rearrange("(q r) c -> r q c", r=4)
+        def blocks(plane):
+            return plane[:].bitcast(I32).rearrange("p (u c) -> p u c", u=2)
 
-        nc.scalar.dma_start(table[0][:], ca_planes[0])
+        def load_scale_rows(queue, staged, src):
+            rows = src[0].bitcast(I32).rearrange("(u v r) c -> v r u c", u=2, r=4)
+            for v in range(2):
+                queue.dma_start(staged[32 * v : 32 * v + 4], rows[v])
+
+        warm = keep.tile([P, 2], F32, name="warm")
+        nc.vector.memset(warm[:, 0:1], 0.0)
+        nc.scalar.activation(warm[:, 1:2], warm[:, 0:1], COPY)
+
+        nc.vector.memset(xo_rows[:], 0)
+        for plane in (w_plane, w2_plane):
+            nc.vector.memset(plane[0:64, :].bitcast(I32), 0)
+        for page in pages:
+            nc.vector.memset(page[:], 0.0)
+
+        nc.sync.dma_start(table[0][:], ca_planes[0])
+        nc.scalar.dma_start(steps[:], sa.rearrange("(p r) o -> p (r o)", r=PACK))
         nc.sync.dma_start(code_list[:], offs)
-        nc.sync.dma_start(steps[:], sa.rearrange("(p r) o -> p (r o)", r=PACK))
-        for r in range(1, PACK):
-            nc.sync.dma_start(table[r][:], ca_planes[r])
-        nc.sync.dma_start(xo_rows[:], scale_rows(xo_scales))
+        nc.sync.dma_start(table[1][:], ca_planes[1])
+        load_scale_rows(nc.sync, xo_rows[:], xo_scales)
         nc.sync.dma_start(token_list[:], offs2)
+        nc.sync.dma_start(table[2][:], ca_planes[2])
+        nc.sync.dma_start(table[3][:], ca_planes[3])
+        load_scale_rows(nc.sync, blocks(w_plane), w_scales)
         nc.sync.dma_start(xo_all[:].bitcast(I32), xo_words[0].bitcast(I32))
+        load_scale_rows(nc.sync, blocks(w2_plane), w2_scales)
         nc.sync.dma_start(w2_codes[:], w2_words[0].rearrange("p n t -> p (n t)").bitcast(I32))
         nc.sync.dma_start(w_codes[:].bitcast(I32), w_words[0].bitcast(I32))
         nc.sync.dma_start(page_list[:], offs3)
-        nc.gpsimd.dma_start(w2_rows[:], scale_rows(w2_scales))
-        nc.gpsimd.dma_start(w_rows[:], scale_rows(w_scales))
         with nc.allow_non_contiguous_dma(reason="one gain a partition"):
-            nc.sync.dma_start(gains[:], so.rearrange("(t p) o -> p (t o)", p=P))
+            nc.gpsimd.dma_start(gains[:], so.rearrange("(t p) o -> p (t o)", p=P))
 
-        for plane in (xo_plane_all, w2_plane, w_plane):
-            nc.vector.memset(plane[:].bitcast(I32), 0)
-        for page in pages:
-            nc.gpsimd.memset(page[:], 0.0)
-
-        def spread(plane, rows):
-            for q in range(4):
-                nc.vector.tensor_copy(plane[32 * q : 32 * q + 4, :].bitcast(I32), rows[:, q, :])
-
-        spread(w2_plane, w2_rows)
-        spread(w_plane, w_rows)
-        spread(xo_plane_all, xo_rows)
+        for u in range(2):
+            nc.vector.tensor_copy(xo_plane_all[64 * u : 64 * (u + 1), :].bitcast(I32), xo_rows[:, u, :])
+        for plane in (w_plane, w2_plane):
+            nc.vector.tensor_copy(blocks(plane)[64:128, 0, :], blocks(plane)[0:64, 1, :])
 
         xo_plane = keep.tile([P, J], U8, name="xo_plane", align_bytes=64)
         nc.vector.tensor_copy(xo_plane[:], xo_plane_all[:].indirect(token_list[:]))
@@ -91,14 +97,14 @@ def tile_list_codesbeside_kernel(tc, ca, sa, xo_words, xo_scales, w_words, w_sca
                 z[h][:, r : PACK * HALF : PACK], table[r][:].indirect(half_list(code_list, h)), COPY, scale=steps[:, r : r + 1]
             )
 
-        for r, h in ((0, 0), (0, 1), (1, 0), (2, 0), (3, 0), (1, 1), (2, 1), (3, 1)):
+        for r, h in [(r, h) for r in range(PACK) for h in range(2)]:
             fetch(r, h)
 
         sums = {}
         for h in range(2):
             xo_codes = keep.tile([P, HALF], U16, name=f"xo_codes{h}", align_bytes=64)
             nc.vector.tensor_copy(xo_codes[:], xo_all[:].indirect(half_list(token_list, h)))
-            z_codes = keep.tile([P, HALF], U32, name=f"z_codes{h}", align_bytes=64)
+            z_codes = keep.tile([P, HALF], U32, name="z_codes", align_bytes=64)
             z_plane = keep.tile([P, HALF], U8, name=f"z_plane{h}", align_bytes=64)
             nc.vector.quantize_mx(out=z_codes[:].bitcast(E4M3X4), scales=z_plane[:], in_=z[h][:])
             for t in range(N // P):

@@ -57,35 +57,38 @@ def tile_list_codesbeside_kernel(tc, ca, sa, xo_words, xo_scales, w_words, w_sca
         nc.scalar.activation(warm[:, 1:2], warm[:, 0:1], COPY)
 
         nc.vector.memset(xo_rows[:], 0)
-        for plane in (w_plane, w2_plane):
+        for plane in (w2_plane, w_plane):
             nc.vector.memset(plane[0:64, :].bitcast(I32), 0)
         for page in pages:
             nc.vector.memset(page[:], 0.0)
 
-        nc.sync.dma_start(table[0][:], ca_planes[0])
         nc.scalar.dma_start(steps[:], sa.rearrange("(p r) o -> p (r o)", r=PACK))
         nc.sync.dma_start(code_list[:], offs)
+        nc.sync.dma_start(table[0][:], ca_planes[0])
         nc.sync.dma_start(table[1][:], ca_planes[1])
         load_scale_rows(nc.sync, xo_rows[:], xo_scales)
         nc.sync.dma_start(token_list[:], offs2)
         nc.sync.dma_start(table[2][:], ca_planes[2])
-        nc.sync.dma_start(table[3][:], ca_planes[3])
-        load_scale_rows(nc.sync, blocks(w_plane), w_scales)
         nc.sync.dma_start(xo_all[:].bitcast(I32), xo_words[0].bitcast(I32))
+        nc.sync.dma_start(table[3][:], ca_planes[3])
         load_scale_rows(nc.sync, blocks(w2_plane), w2_scales)
-        nc.sync.dma_start(w2_codes[:], w2_words[0].rearrange("p n t -> p (n t)").bitcast(I32))
-        nc.sync.dma_start(w_codes[:].bitcast(I32), w_words[0].bitcast(I32))
+        load_scale_rows(nc.sync, blocks(w_plane), w_scales)
         nc.sync.dma_start(page_list[:], offs3)
+        nc.gpsimd.dma_start(w2_codes[:], w2_words[0].rearrange("p n t -> p (n t)").bitcast(I32))
+        nc.gpsimd.dma_start(w_codes[:].bitcast(I32), w_words[0].bitcast(I32))
         with nc.allow_non_contiguous_dma(reason="one gain a partition"):
-            nc.gpsimd.dma_start(gains[:], so.rearrange("(t p) o -> p (t o)", p=P))
+            nc.sync.dma_start(gains[:], so.rearrange("(t p) o -> p (t o)", p=P))
 
         for u in range(2):
             nc.vector.tensor_copy(xo_plane_all[64 * u : 64 * (u + 1), :].bitcast(I32), xo_rows[:, u, :])
-        for plane in (w_plane, w2_plane):
+        for plane in (w2_plane, w_plane):
             nc.vector.tensor_copy(blocks(plane)[64:128, 0, :], blocks(plane)[0:64, 1, :])
 
         xo_plane = keep.tile([P, J], U8, name="xo_plane", align_bytes=64)
         nc.vector.tensor_copy(xo_plane[:], xo_plane_all[:].indirect(token_list[:]))
+
+        xo_codes = keep.tile([P, J], U16, name="xo_codes", align_bytes=64)
+        nc.vector.tensor_copy(xo_codes[:], xo_all[:].indirect(token_list[:]))
 
         def half_list(lst, h):
             return lst[:, h * LIST_COLS // 2 : (h + 1) * LIST_COLS // 2]
@@ -102,31 +105,26 @@ def tile_list_codesbeside_kernel(tc, ca, sa, xo_words, xo_scales, w_words, w_sca
 
         sums = {}
         for h in range(2):
-            xo_codes = keep.tile([P, HALF], U16, name=f"xo_codes{h}", align_bytes=64)
-            nc.vector.tensor_copy(xo_codes[:], xo_all[:].indirect(half_list(token_list, h)))
             z_codes = keep.tile([P, HALF], U32, name="z_codes", align_bytes=64)
             z_plane = keep.tile([P, HALF], U8, name=f"z_plane{h}", align_bytes=64)
             nc.vector.quantize_mx(out=z_codes[:].bitcast(E4M3X4), scales=z_plane[:], in_=z[h][:])
             for t in range(N // P):
                 acc = psum.tile([P, HALF], F32, name=f"acc{h}{t}")
-                nc.tensor.matmul_mx(
-                    out=acc[:],
+                token_pass = dict(
                     lhsT=w2_codes[:, t * P : (t + 1) * P].bitcast(E5M2X4),
                     lhsT_scale=w2_plane[:, t * P : (t + 1) * P],
-                    rhs=xo_codes[:].bitcast(E2M1X4),
+                    rhs=xo_codes[:, h * HALF : (h + 1) * HALF].bitcast(E2M1X4),
                     rhs_scale=xo_plane[:, h * HALF : (h + 1) * HALF],
-                    start=True,
-                    stop=False,
                 )
-                nc.tensor.matmul_mx(
-                    out=acc[:],
+                code_pass = dict(
                     lhsT=w_codes[:, 2 * t * P : 2 * (t + 1) * P].bitcast(E2M1X4),
                     lhsT_scale=w_plane[:, t * P : (t + 1) * P],
                     rhs=z_codes[:].bitcast(E4M3X4),
                     rhs_scale=z_plane[:],
-                    start=False,
-                    stop=True,
                 )
+                first, second = (token_pass, code_pass) if h == 0 else (code_pass, token_pass)
+                nc.tensor.matmul_mx(out=acc[:], start=True, stop=False, **first)
+                nc.tensor.matmul_mx(out=acc[:], start=False, stop=True, **second)
                 p_rows = keep.tile([P, HALF], F32, name=f"p_rows{h}{t}")
                 nc.vector.tensor_copy(p_rows[:], acc[:])
                 sums[h, t] = p_rows

from contextlib import ExitStack

import concourse.mybir as mybir

F32 = mybir.dt.float32
BF16 = mybir.dt.bfloat16
I32 = mybir.dt.int32
U32 = mybir.dt.uint32
U16 = mybir.dt.uint16
U8 = mybir.dt.uint8
E4M3X4 = mybir.dt.float8_e4m3fn_x4
E5M2X4 = mybir.dt.float8_e5m2_x4
E2M1X4 = mybir.dt.float4_e2m1fn_x4
COPY = mybir.ActivationFunctionType.Copy

P = 128
PACK = 4
K, T, F, Z, J, N, E = 512, 512, 512, 1024, 256, 256, 512
HALF = J // 2
LIST_COLS = J // 16
FLOPS = 2 * K * N * J + 2 * F * N * J


def tile_list_codesbeside_kernel(tc, ca, sa, xo_words, xo_scales, w_words, w_scales, w2_words, w2_scales, so, offs, offs2, offs3, out):
    nc = tc.nc
    with ExitStack() as ctx:
        keep = ctx.enter_context(tc.tile_pool(name="keep", bufs=1))
        psum = ctx.enter_context(tc.psum_pool(name="psum", bufs=1))

        code_list = keep.tile([P, LIST_COLS], U16, name="code_list")
        token_list = keep.tile([P, LIST_COLS], U16, name="token_list")
        page_list = keep.tile([P, LIST_COLS], U16, name="page_list")
        steps = keep.tile([P, PACK], F32, name="steps")
        gains = keep.tile([P, N // P], F32, name="gains")
        table = [keep.tile([P, T], F32, name=f"table{r}") for r in range(PACK)]
        xo_all = keep.tile([P, Z], U16, name="xo_all", align_bytes=64)
        w_codes = keep.tile([P, 2 * N], U8, name="w_codes", align_bytes=64)
        w2_codes = keep.tile([P, N], I32, name="w2_codes", align_bytes=64)
        xo_rows = keep.tile([64, 2, Z // 4], I32, name="xo_rows")
        xo_plane_all = keep.tile([P, Z], U8, name="xo_plane_all", align_bytes=64)
        w_plane = keep.tile([P, 2 * N], U8, name="w_plane", align_bytes=64)
        w2_plane = keep.tile([P, 2 * N], U8, name="w2_plane", align_bytes=64)
        pages = [keep.tile([P, E], F32, name=f"page{t}") for t in range(N // P)]

        ca_planes = ca.rearrange("(p r) t -> r p t", r=PACK)

        def blocks(plane):
            return plane[:].bitcast(I32).rearrange("p (u c) -> p u c", u=2)

        def load_scale_rows(queue, staged, src):
            rows = src[0].bitcast(I32).rearrange("(u v r) c -> v r u c", u=2, r=4)
            for v in range(2):
                queue.dma_start(staged[32 * v : 32 * v + 4], rows[v])

        warm = keep.tile([P, 2], F32, name="warm")
        nc.vector.memset(warm[:, 0:1], 0.0)
        nc.scalar.activation(warm[:, 1:2], warm[:, 0:1], COPY)

        nc.vector.memset(xo_rows[:], 0)
        for plane in (w2_plane, w_plane):
            nc.vector.memset(plane[0:64, :].bitcast(I32), 0)
        for page in pages:
            nc.vector.memset(page[:], 0.0)

        nc.scalar.dma_start(steps[:], sa.rearrange("(p r) o -> p (r o)", r=PACK))
        nc.sync.dma_start(code_list[:], offs)
        nc.sync.dma_start(table[0][:], ca_planes[0])
        nc.sync.dma_start(table[1][:], ca_planes[1])
        load_scale_rows(nc.sync, xo_rows[:], xo_scales)
        nc.sync.dma_start(token_list[:], offs2)
        nc.sync.dma_start(table[2][:], ca_planes[2])
        nc.sync.dma_start(xo_all[:].bitcast(I32), xo_words[0].bitcast(I32))
        nc.sync.dma_start(table[3][:], ca_planes[3])
        load_scale_rows(nc.sync, blocks(w2_plane), w2_scales)
        load_scale_rows(nc.sync, blocks(w_plane), w_scales)
        nc.sync.dma_start(page_list[:], offs3)
        nc.gpsimd.dma_start(w2_codes[:], w2_words[0].rearrange("p n t -> p (n t)").bitcast(I32))
        nc.gpsimd.dma_start(w_codes[:].bitcast(I32), w_words[0].bitcast(I32))
        with nc.allow_non_contiguous_dma(reason="one gain a partition"):
            nc.sync.dma_start(gains[:], so.rearrange("(t p) o -> p (t o)", p=P))

        for u in range(2):
            nc.vector.tensor_copy(xo_plane_all[64 * u : 64 * (u + 1), :].bitcast(I32), xo_rows[:, u, :])
        for plane in (w2_plane, w_plane):
            nc.vector.tensor_copy(blocks(plane)[64:128, 0, :], blocks(plane)[0:64, 1, :])

        xo_plane = keep.tile([P, J], U8, name="xo_plane", align_bytes=64)
        nc.vector.tensor_copy(xo_plane[:], xo_plane_all[:].indirect(token_list[:]))

        xo_codes = keep.tile([P, J], U16, name="xo_codes", align_bytes=64)
        nc.vector.tensor_copy(xo_codes[:], xo_all[:].indirect(token_list[:]))

        def half_list(lst, h):
            return lst[:, h * LIST_COLS // 2 : (h + 1) * LIST_COLS // 2]

        z = [keep.tile([P, PACK * HALF], BF16, name=f"z{h}", align_bytes=64) for h in range(2)]

        def fetch(r, h):
            nc.scalar.activation(
                z[h][:, r : PACK * HALF : PACK], table[r][:].indirect(half_list(code_list, h)), COPY, scale=steps[:, r : r + 1]
            )

        for r, h in [(r, h) for r in range(PACK) for h in range(2)]:
            fetch(r, h)

        sums = {}
        for h in range(2):
            z_codes = keep.tile([P, HALF], U32, name="z_codes", align_bytes=64)
            z_plane = keep.tile([P, HALF], U8, name=f"z_plane{h}", align_bytes=64)
            nc.vector.quantize_mx(out=z_codes[:].bitcast(E4M3X4), scales=z_plane[:], in_=z[h][:])
            for t in range(N // P):
                acc = psum.tile([P, HALF], F32, name=f"acc{h}{t}")
                token_pass = dict(
                    lhsT=w2_codes[:, t * P : (t + 1) * P].bitcast(E5M2X4),
                    lhsT_scale=w2_plane[:, t * P : (t + 1) * P],
                    rhs=xo_codes[:, h * HALF : (h + 1) * HALF].bitcast(E2M1X4),
                    rhs_scale=xo_plane[:, h * HALF : (h + 1) * HALF],
                )
                code_pass = dict(
                    lhsT=w_codes[:, 2 * t * P : 2 * (t + 1) * P].bitcast(E2M1X4),
                    lhsT_scale=w_plane[:, t * P : (t + 1) * P],
                    rhs=z_codes[:].bitcast(E4M3X4),
                    rhs_scale=z_plane[:],
                )
                first, second = (token_pass, code_pass) if h == 0 else (code_pass, token_pass)
                nc.tensor.matmul_mx(out=acc[:], start=True, stop=False, **first)
                nc.tensor.matmul_mx(out=acc[:], start=False, stop=True, **second)
                p_rows = keep.tile([P, HALF], F32, name=f"p_rows{h}{t}")
                nc.vector.tensor_copy(p_rows[:], acc[:])
                sums[h, t] = p_rows

        for h in range(2):
            for t in range(N // P):
                nc.scalar.activation(pages[t][:].indirect(half_list(page_list, h)), sums[h, t][:], COPY, scale=gains[:, t : t + 1])
        for t in range(N // P):
            nc.sync.dma_start(out[t * P : (t + 1) * P, :], pages[t][:])
